import numpy as np
import ml_dtypes


def mxq(x, axis, fmt="e4m3"):
    dtype, down = {"e4m3": (ml_dtypes.float8_e4m3fn, 7), "e5m2": (ml_dtypes.float8_e5m2, 14)}[fmt]
    v = np.moveaxis(np.asarray(x, np.float32).astype(ml_dtypes.bfloat16).astype(np.float64), axis, -1)
    blocks = v.reshape(v.shape[:-1] + (-1, 32))
    amax = np.abs(blocks).max(-1, keepdims=True)
    byte = np.maximum(np.where(amax > 0, np.frexp(amax)[1] - 1 + 127, 0) - down, 1)
    scale = np.exp2(byte - 127.0)
    codes = (blocks / scale).astype(np.float32).astype(dtype).astype(np.float64)
    return np.moveaxis((codes * scale).reshape(v.shape), -1, axis)


WIDE = False


def mx_kscale(k):
    if not WIDE:
        return np.ones(k)
    levels = np.array([10, -10, 5, -5, 0])
    if k % 512:
        return np.exp2(np.random.permutation(np.resize(levels, k // 32))).repeat(32)
    a = np.empty((k // 512, 16))
    for p in range(k // 512):
        a[p, :8] = np.random.permutation(np.resize(levels, 8))
        for g in range(8):
            far = levels[np.abs(levels - a[p, g]) >= 10]
            a[p, g + 8] = far[np.random.randint(len(far))]
    return np.exp2(a.ravel()).repeat(32)


def f64(x):
    return np.asarray(x).astype(np.float64)


def striped(idx):
    return np.tile(idx.reshape(-1, 16).T, (8, 1)).astype(np.uint16)


def unstriped(offs):
    return offs[:16].T.reshape(-1).astype(np.int64)


def striped8(idx):
    return np.concatenate([x.reshape(-1, 16).T for x in idx]).astype(np.uint16)


def runs(offs, k):
    lists = np.stack([offs[16 * r : 16 * r + 16].T.reshape(-1) for r in range(8)]).astype(np.int64)
    return lists[np.arange(k) % 512 // 64]


def pack_weight(w):
    k, n = w.shape
    w = f64(np.asarray(w, np.float32).astype(ml_dtypes.bfloat16)).reshape(k // 32, 32, n)
    amax = np.abs(w).max(1)
    byte = np.clip(np.where(amax > 0, np.frexp(amax)[1] - 1 + 127 - 7, 1), 1, 254)
    scaled = (w * np.exp2(127.0 - byte)[:, None, :]).reshape(k, n).astype(np.float32)
    words = np.ascontiguousarray(scaled.reshape(k // 512, 128, 4, n).transpose(0, 1, 3, 2)).astype(ml_dtypes.float8_e4m3fn).view(np.uint8)
    return words, np.ascontiguousarray(byte.astype(np.uint8).reshape(k // 512, 16, n))


def unpack_weight(words, scales):
    g, p, n, _ = words.shape
    vals = np.ascontiguousarray(words).view(ml_dtypes.float8_e4m3fn).astype(np.float64) * np.repeat(np.exp2(scales.astype(np.float64) - 127.0), 8, axis=1)[..., None]
    return vals.transpose(0, 1, 3, 2).reshape(g * 512, n)


def sigmoid(v):
    return 1.0 / (1.0 + np.exp(-np.maximum(v, -700.0)))


K, T, S, N, H = 512, 2048, 512, 512, 512


def setup_inputs():
    n = np.random.standard_normal
    s = mx_kscale(K)[:, None]
    u = mx_kscale(H)
    packed_xT = pack_weight(n((K, T)) * s)
    return {
        "x_words": packed_xT[0],
        "x_scales": packed_xT[1],
        "w1": (n((K, H)) / np.sqrt(K) / s).astype(np.float32),
        "w2": (n((K, H)) / np.sqrt(K) / s).astype(np.float32),
        "gn": (np.random.uniform(0.5, 1.5, (H, 1)) * u[:, None]).astype(np.float32),
        "gm": (np.random.uniform(0.5, 1.5, (H, 1)) * u[:, None]).astype(np.float32),
        "w3": (n((H, N)) / np.sqrt(2 * H) / u[:, None]).astype(np.float32),
        "w4": (n((H, N)) / np.sqrt(2 * H) / u[:, None]).astype(np.float32),
        "offs": striped(np.random.permutation(T)[:S]),
        "hz": striped8(np.random.randint(0, T, (8, S))),
        "n1": striped(np.random.permutation(S)),
        "n2": striped(np.random.permutation(S)),
        "n3": striped8(np.stack([np.random.permutation(S) for _ in range(8)])),
        "n4": striped8(np.stack([np.random.permutation(S) for _ in range(8)])),
        "n5": striped(np.random.permutation(S)),
        "n6": striped(np.random.permutation(S)),
    }


def reference(x_words, x_scales, w1, w2, gn, gm, w3, w4, offs, hz, n1, n2, n3, n4, n5, n6):
    xq = unpack_weight(x_words, x_scales)[:, unstriped(offs)]
    y = mxq(f64(w1), 0, "e4m3").T @ xq
    z = f64(gn) * (y * (y[:, unstriped(n1)] - y[:, unstriped(n2)]))
    x_hz = unpack_weight(x_words, x_scales)[np.arange(K)[:, None], runs(hz, K)]
    d = mxq(f64(w2), 0, "e4m3").T @ x_hz
    pa = d[np.arange(H)[:, None], runs(n3, H)]
    pb = d[np.arange(H)[:, None], runs(n4, H)]
    mu = 0.3125 * (d + pa + pb)
    z2 = f64(gm) * ((d - mu) / (np.sqrt((pa - mu) ** 2 + (pb - mu) ** 2 + 0.25)))
    h = mxq(f64(w3), 0, "e4m3").T @ mxq(z, 0, "e4m3") + mxq(f64(w4), 0, "e4m3").T @ mxq(z2, 0, "e4m3")
    return h + (sigmoid(h[:, unstriped(n5)])) * (h[:, unstriped(n6)] - h)

@@ -1,0 +1,319 @@
+from contextlib import ExitStack
+
+import concourse.mybir as mybir
+from concourse.masks import make_identity
+
+K, T, S, N, H = 512, 2048, 512, 512, 512
+FLOPS = 4 * 2 * 512 * 512 * 512
+
+F32 = mybir.dt.float32
+BF16 = mybir.dt.bfloat16
+I32 = mybir.dt.int32
+U32 = mybir.dt.uint32
+U16 = mybir.dt.uint16
+U8 = mybir.dt.uint8
+FP8X4 = mybir.dt.float8_e4m3fn_x4
+ACT = mybir.ActivationFunctionType
+ALU = mybir.AluOpType
+
+P = 128
+PACK = 4
+HALF = S // 2
+
+
+def tile_picked_hjoinwindstdtrack_none_p_kernel(
+    tc, x_words, x_scales, w1, w2, gn, gm, w3, w4, offs, hz, n1, n2, n3, n4, n5, n6, out
+):
+    nc = tc.nc
+    with ExitStack() as ctx:
+        sb = ctx.enter_context(tc.tile_pool(name="sb", bufs=1))
+        ring = ctx.enter_context(tc.tile_pool(name="ring", bufs=4))
+        ps = ctx.enter_context(tc.psum_pool(name="ps", bufs=4))
+        ps_y = ctx.enter_context(tc.psum_pool(name="ps_y", bufs=4))
+
+        def load_list(name, src):
+            tile = sb.tile([P, S // 16], U16, name=name)
+            nc.sync.dma_start(tile[:], src)
+            return tile
+
+        def load_weight_half(name, w, half):
+            raw = sb.tile([P, PACK, HALF], F32, name=name)
+            cols = slice(half * HALF, (half + 1) * HALF)
+            nc.sync.dma_start(raw[:], w.rearrange("(p j) c -> p j c", j=PACK)[:, :, cols])
+            return raw
+
+        def half_list(tile, half):
+            return tile[:, half * HALF // 16 : (half + 1) * HALF // 16]
+
+        def copy_on(engine, dst, src):
+            if engine == "scalar":
+                nc.scalar.copy(dst, src)
+            else:
+                nc.vector.tensor_copy(dst, src)
+
+        def round_dealt(grouped, raw, half, engine):
+            dst = grouped[:].rearrange("p (t m j) -> p m j t", t=PACK, j=PACK)[:, half * 64 : (half + 1) * 64]
+            copy_on(engine, dst, raw[:].rearrange("p j (m t) -> p m j t", t=PACK))
+
+        def round_plain(grouped, raw, half, engine):
+            dst = grouped[:].rearrange("p (c i j) -> p c j i", i=4, j=PACK)[:, half * 64 : (half + 1) * 64]
+            copy_on(engine, dst, raw[:].rearrange("p j (c i) -> p c j i", i=4))
+
+        def quantize(name, grouped, pieces=1):
+            codes = sb.tile([P, 512], U32, name=name + "_codes", align_bytes=64)
+            scales = sb.tile([P, 512], U8, name=name + "_scales", align_bytes=64)
+            width = 512 // pieces
+            for i in range(pieces):
+                cols = slice(i * width, (i + 1) * width)
+                nc.vector.quantize_mx(
+                    out=codes[:, cols].bitcast(FP8X4),
+                    scales=scales[:, cols],
+                    in_=grouped[:, PACK * i * width : PACK * (i + 1) * width],
+                )
+            return codes, scales
+
+        def mx(acc, lhs, lcols, rhs, rcols, start=True, stop=True):
+            nc.tensor.matmul_mx(
+                out=acc,
+                lhsT=lhs[0][:, lcols].bitcast(FP8X4),
+                lhsT_scale=lhs[1][:, lcols],
+                rhs=rhs[0][:, rcols].bitcast(FP8X4),
+                rhs_scale=rhs[1][:, rcols],
+                start=start,
+                stop=stop,
+            )
+
+        def blk(i):
+            return slice(i * P, (i + 1) * P)
+
+        hz_l = load_list("hz_l", hz)
+        x_bytes = sb.tile([P, T], U8, name="x_bytes", tag="bytes_then_codes", align_bytes=64)
+        rows = x_scales[0].bitcast(I32)
+        for q in range(4):
+            src = rows[4 * q : 4 * q + 4, :].unsqueeze(0).to_broadcast([8, 4, T // 4])
+            queue = nc.sync if q < 2 else nc.scalar
+            queue.dma_start(x_bytes[32 * q : 32 * q + 32, :].bitcast(I32), src)
+        offs_l = load_list("offs_l", offs)
+        x_codes = sb.tile([P, T], U32, name="x_codes")
+        nc.sync.dma_start(x_codes[:].bitcast(I32), x_words[0].rearrange("p c r -> p (c r)").bitcast(I32))
+        w2_raw = [load_weight_half("wa%d" % h, w2, h) for h in range(2)]
+        gm_sb = sb.tile([P, PACK], F32, name="gm_sb")
+        nc.sync.dma_start(gm_sb[:], gm.rearrange("(p t) o -> p (t o)", t=PACK))
+        n3_l = load_list("n3_l", n3)
+        n4_l = load_list("n4_l", n4)
+        w1_raw = [load_weight_half("wb%d" % h, w1, h) for h in range(2)]
+        gn_sb = sb.tile([P, PACK], F32, name="gn_sb")
+        nc.sync.dma_start(gn_sb[:], gn.rearrange("(p t) o -> p (t o)", t=PACK))
+        n1_l = load_list("n1_l", n1)
+        n2_l = load_list("n2_l", n2)
+
+        ident = sb.tile([P, P], F32, name="ident")
+        make_identity(nc, ident[:])
+
+        hz_bytes = sb.tile([P, S], U8, name="hz_bytes", align_bytes=64)
+        nc.vector.tensor_copy(hz_bytes[:], x_bytes[:].indirect(hz_l[:]))
+        hz_scales = sb.tile([P, S], U8, name="hz_scales", align_bytes=64)
+        nc.vector.tensor_copy(hz_scales[:].bitcast(I32), hz_bytes[:].bitcast(I32))
+        for r in (2, 3):
+            nc.scalar.dma_start(hz_scales[r:P:32, :].bitcast(I32), hz_bytes[16 + r : P : 32, :].bitcast(I32))
+        offs_scales = sb.tile([P, S], U8, name="offs_scales", align_bytes=64)
+        nc.vector.tensor_copy(offs_scales[:], x_bytes[:].indirect(offs_l[:]))
+
+        hz_codes = sb.tile([P, S], U32, name="hz_codes", tag="bytes_then_codes", align_bytes=64)
+        nc.vector.tensor_copy(hz_codes[:], x_codes[:].indirect(hz_l[:]))
+        offs_codes = sb.tile([P, S], U32, name="offs_codes", align_bytes=64)
+        nc.vector.tensor_copy(offs_codes[:], x_codes[:].indirect(offs_l[:]))
+
+        gw = sb.tile([P, PACK], F32, name="gw")
+        nc.vector.tensor_scalar(gw[:], gm_sb[:], 0.6875, None, ALU.mult)
+        gzero = sb.tile([P, PACK], F32, name="gzero")
+        nc.vector.tensor_scalar(gzero[:], gm_sb[:], 0.0, None, ALU.is_equal)
+        w2_g = sb.tile([P, 2048], BF16, name="w2_g", align_bytes=64)
+        round_dealt(w2_g, w2_raw[0], 0, "scalar")
+        round_dealt(w2_g, w2_raw[1], 1, "vector")
+        w2_q = quantize("w2", w2_g, 2)
+        d_acc = []
+        for t in range(PACK):
+            acc = ps.tile([P, S], F32, name="d_acc", tag="bank")
+            mx(acc[:], w2_q, blk(t), (hz_codes, hz_scales), slice(0, S))
+            d_acc.append(acc)
+
+        gsafe = sb.tile([P, PACK], F32, name="gsafe")
+        nc.vector.tensor_tensor(gsafe[:], gw[:], gzero[:], ALU.add)
+        ginv = sb.tile([P, PACK], F32, name="ginv")
+        nc.vector.reciprocal(ginv[:], gsafe[:])
+        qscale = sb.tile([P, PACK], F32, name="qscale")
+        nc.vector.scalar_tensor_tensor(qscale[:], ginv[:], 0.1953125, ginv[:], ALU.mult, ALU.mult)
+        quarter = sb.tile([P, 1], F32, name="quarter")
+        nc.vector.memset(quarter[:], 0.25)
+
+        num = sb.tile([P, PACK, S], F32, name="num")
+        rinv = sb.tile([P, PACK, S], F32, name="rinv")
+        diff = sb.tile([P, PACK, S], F32, name="diff")
+
+        d_win = [sb.tile([P, S], F32, name="d_win%d" % t) for t in range(PACK)]
+        y_win = sb.tile([P, PACK, S], F32, name="y_win")
+
+        def turned_sum(acc, terms):
+            for c in range(2):
+                for i, term in enumerate(terms):
+                    nc.tensor.matmul(
+                        acc[:, blk(c)], term[:, blk(c)], ident[:],
+                        start=(i == 0), stop=(i == len(terms) - 1), is_transpose=True,
+                    )
+
+        def half_cols(h):
+            return slice(h * HALF, (h + 1) * HALF)
+
+        def track_front(t, h):
+            win = d_win[t]
+            if h == 0:
+                nc.scalar.activation(win[:], d_acc[t][:], ACT.Copy, scale=gw[:, t : t + 1])
+            a = ring.tile([P, HALF], F32, name="a")
+            b = ring.tile([P, HALF], F32, name="b")
+            nc.scalar.activation(a[:], win[:].indirect(half_list(n3_l, h)), ACT.Copy, scale=-0.6)
+            nc.vector.tensor_scalar(b[:], win[:].indirect(half_list(n4_l, h)), 0.6, 0.0, ALU.mult, ALU.add)
+            s = ring.tile([P, HALF], F32, name="s")
+            nc.vector.tensor_tensor(s[:], a[:], b[:], ALU.subtract)
+            tu_acc = ps.tile([P, 2, HALF], F32, name="tu_acc", tag="bank")
+            turned_sum(tu_acc[:, 0, :], [a, b])
+            turned_sum(tu_acc[:, 1, :], [s, win[:, half_cols(h)]])
+            return tu_acc, s
+
+        def track_back(t, h, tu_acc, s):
+            cols = half_cols(h)
+            nc.vector.scalar_tensor_tensor(num[:, t, cols], s[:], 25.0 / 33.0, d_win[t][:, cols], ALU.mult, ALU.add)
+            t2 = ring.tile([P, HALF], F32, name="t2")
+            nc.scalar.activation(t2[:], tu_acc[:, 0, :], ACT.Square, scale=8.0 / 3.0)
+            u2 = ring.tile([P, HALF], F32, name="u2")
+            nc.scalar.activation(u2[:], tu_acc[:, 1, :], ACT.Square)
+            q_acc = ps.tile([P, HALF], F32, name="q_acc", tag="bank")
+            turned_sum(q_acc, [t2, u2])
+            return q_acc
+
+        def track_root(t, h, q_acc):
+            nc.scalar.activation(
+                rinv[:, t, half_cols(h)], q_acc[:], ACT.Abs_reciprocal_sqrt, bias=quarter[:], scale=qscale[:, t : t + 1]
+            )
+
+        def wind(t, h):
+            y1 = ring.tile([P, HALF], F32, name="y1", bufs=2)
+            y2 = ring.tile([P, HALF], F32, name="y2", bufs=2)
+            nc.scalar.activation(y1[:], y_win[:, t, :].indirect(half_list(n1_l, h)), ACT.Copy)
+            nc.scalar.activation(y2[:], y_win[:, t, :].indirect(half_list(n2_l, h)), ACT.Copy)
+            nc.vector.tensor_tensor(diff[:, t, half_cols(h)], y1[:], y2[:], ALU.subtract)
+
+        def woven(ap):
+            return ap.rearrange("p t (c i) -> p c t i", i=4)
+
+        def weave(tile, c0, c1):
+            return tile[:].rearrange("p (c i t) -> p c t i", i=4, t=PACK)[:, 32 * c0 : 32 * c1]
+
+        def quantize_half(q, grouped, h):
+            nc.vector.quantize_mx(
+                out=q[0][:, h * HALF : (h + 1) * HALF].bitcast(FP8X4),
+                scales=q[1][:, h * HALF : (h + 1) * HALF],
+                in_=grouped[:, h * 1024 : (h + 1) * 1024],
+            )
+
+        w4_g = sb.tile([P, 2048], BF16, name="w4_g", align_bytes=64)
+        w3_g = sb.tile([P, 2048], BF16, name="w3_g", align_bytes=64)
+        z2_g = sb.tile([P, 2048], BF16, name="z2_g", align_bytes=64)
+        z_g = sb.tile([P, 2048], BF16, name="z_g", align_bytes=64)
+        z_q = (
+            sb.tile([P, 512], U32, name="z_codes", align_bytes=64),
+            sb.tile([P, 512], U8, name="z_scales", align_bytes=64),
+        )
+
+        z2_q = (
+            sb.tile([P, 512], U32, name="z2_codes", align_bytes=64),
+            sb.tile([P, 512], U8, name="z2_scales", align_bytes=64),
+        )
+        y_acc = []
+
+        def project_y():
+            w1_g = sb.tile([P, 2048], BF16, name="w1_g", align_bytes=64)
+            round_dealt(w1_g, w1_raw[0], 0, "scalar")
+            round_dealt(w1_g, w1_raw[1], 1, "vector")
+            w1_q = quantize("w1", w1_g)
+            for c in range(4):
+                acc = ps_y.tile([P, PACK, P], F32, name="y_acc")
+                for t in range(PACK):
+                    mx(acc[:, t, :], w1_q, blk(t), (offs_codes, offs_scales), blk(c))
+                nc.vector.tensor_tensor(
+                    y_win[:, :, blk(c)], acc[:], gn_sb[:].unsqueeze(2).to_broadcast([P, PACK, P]), ALU.mult
+                )
+                y_acc.append(acc)
+
+        def wind_product(h):
+            for c in (2 * h, 2 * h + 1):
+                nc.vector.tensor_tensor(weave(z_g, c, c + 1), woven(y_acc[c][:]), woven(diff[:, :, blk(c)]), ALU.mult)
+
+        def track_product(h):
+            cols = half_cols(h)
+            nc.vector.tensor_tensor(weave(z2_g, 2 * h, 2 * h + 2), woven(num[:, :, cols]), woven(rinv[:, :, cols]), ALU.mult)
+
+        units = [(t, h) for h in range(2) for t in range(PACK)]
+        fronts, sums = {}, {}
+        for step in range(len(units) + 4):
+            if step < len(units):
+                fronts[step] = track_front(*units[step])
+            if step == 1:
+                project_y()
+                w4_raw = [load_weight_half("wa%d" % h, w4, h) for h in range(2)]
+                w3_raw = [load_weight_half("wb%d" % h, w3, h) for h in range(2)]
+                n5_l = load_list("n5_l", n5)
+                n6_l = load_list("n6_l", n6)
+            if 0 <= step - 2 < len(units):
+                sums[step - 2] = track_back(*units[step - 2], *fronts[step - 2])
+            if 0 <= step - 4 < len(units):
+                wind(*units[step - 4])
+            if 0 <= step - 3 < len(units):
+                track_root(*units[step - 3], sums[step - 3])
+            if step == 5:
+                for h in range(2):
+                    round_plain(w4_g, w4_raw[h], h, "vector")
+            if step == 6:
+                w4_q = quantize("w4", w4_g)
+            if step == 7:
+                track_product(0)
+            if step == 8:
+                wind_product(0)
+                quantize_half(z2_q, z2_g, 0)
+            if step == 9:
+                for h in range(2):
+                    round_plain(w3_g, w3_raw[h], h, "vector")
+                quantize_half(z_q, z_g, 0)
+            if step == 10:
+                w3_q = quantize("w3", w3_g)
+                track_product(1)
+        quantize_half(z2_q, z2_g, 1)
+        wind_product(1)
+        quantize_half(z_q, z_g, 1)
+
+        h_acc = []
+        for m in range(4):
+            acc = ps.tile([P, S], F32, name="h_acc", tag="bank")
+            mx(acc[:], w4_q, blk(m), z2_q, slice(0, S), True, False)
+            h_acc.append(acc)
+        for m in range(4):
+            mx(h_acc[m][:], w3_q, blk(m), z_q, slice(0, S), False, True)
+        for m in range(4):
+            h_win = sb.tile([P, S], F32, name="h_win%d" % m)
+            nc.vector.tensor_copy(h_win[:], h_acc[m][:])
+            gate = ring.tile([P, S], F32, name="gate")
+            far = ring.tile([P, S], F32, name="far")
+            step = ring.tile([P, S], F32, name="step")
+            gated = ring.tile([P, S], F32, name="gated")
+            res = sb.tile([P, S], F32, name="res%d" % m)
+            halves = [slice(h * HALF, (h + 1) * HALF) for h in range(2)]
+            for h, cols in enumerate(halves):
+                nc.scalar.activation(gate[:, cols], h_win[:].indirect(half_list(n5_l, h)), ACT.Sigmoid)
+                nc.scalar.activation(far[:, cols], h_win[:].indirect(half_list(n6_l, h)), ACT.Copy)
+            for cols in halves:
+                nc.vector.tensor_tensor(step[:, cols], far[:, cols], h_win[:, cols], ALU.subtract)
+            for cols in halves:
+                nc.vector.tensor_tensor(gated[:, cols], step[:, cols], gate[:, cols], ALU.mult)
+            for cols in halves:
+                nc.vector.tensor_tensor(res[:, cols], gated[:, cols], h_win[:, cols], ALU.add)
+                nc.sync.dma_start(out[blk(m), cols], res[:, cols])

@@ -19,6 +19,10 @@ ALU = mybir.AluOpType
 P = 128
 PACK = 4
 HALF = S // 2
+W0 = ["vector", "scalar", "scalar", "scalar"]
+W1 = ["scalar", "scalar", "scalar", "scalar"]
+B_ON_SCALAR = [(3, 1)]
+FAR_ON_VECTOR = [(0, 0), (2, 0)]
 
 
 def tile_picked_hjoinwindstdtrack_none_p_kernel(
@@ -37,7 +41,7 @@ def tile_picked_hjoinwindstdtrack_none_p_kernel(
             return tile
 
         def load_weight_half(name, w, half):
-            raw = sb.tile([P, PACK, HALF], F32, name=name)
+            raw = sb.tile([P, PACK, HALF], F32, name=name, align_bytes=64)
             cols = slice(half * HALF, (half + 1) * HALF)
             nc.sync.dma_start(raw[:], w.rearrange("(p j) c -> p j c", j=PACK)[:, :, cols])
             return raw
@@ -53,11 +57,11 @@ def tile_picked_hjoinwindstdtrack_none_p_kernel(
 
         def round_dealt(grouped, raw, half, engine):
             dst = grouped[:].rearrange("p (t m j) -> p m j t", t=PACK, j=PACK)[:, half * 64 : (half + 1) * 64]
-            copy_on(engine, dst, raw[:].rearrange("p j (m t) -> p m j t", t=PACK))
+            copy_on(engine, dst, raw[half][:].rearrange("p j (m t) -> p m j t", t=PACK))
 
         def round_plain(grouped, raw, half, engine):
             dst = grouped[:].rearrange("p (c i j) -> p c j i", i=4, j=PACK)[:, half * 64 : (half + 1) * 64]
-            copy_on(engine, dst, raw[:].rearrange("p j (c i) -> p c j i", i=4))
+            copy_on(engine, dst, raw[half][:].rearrange("p j (c i) -> p c j i", i=4))
 
         def quantize(name, grouped, pieces=1):
             codes = sb.tile([P, 512], U32, name=name + "_codes", align_bytes=64)
@@ -86,19 +90,20 @@ def tile_picked_hjoinwindstdtrack_none_p_kernel(
         def blk(i):
             return slice(i * P, (i + 1) * P)
 
-        hz_l = load_list("hz_l", hz)
         x_bytes = sb.tile([P, T], U8, name="x_bytes", tag="bytes_then_codes", align_bytes=64)
-        rows = x_scales[0].bitcast(I32)
-        for q in range(4):
-            src = rows[4 * q : 4 * q + 4, :].unsqueeze(0).to_broadcast([8, 4, T // 4])
-            queue = nc.sync if q < 2 else nc.scalar
-            queue.dma_start(x_bytes[32 * q : 32 * q + 32, :].bitcast(I32), src)
+        nc.gpsimd.memset(x_bytes[:].bitcast(I32), 0)
+        hz_l = load_list("hz_l", hz)
+        gm_sb = sb.tile([P, PACK], F32, name="gm_sb")
+        nc.scalar.dma_start(gm_sb[:], gm.rearrange("(p t) o -> p (t o)", t=PACK))
         offs_l = load_list("offs_l", offs)
+        rows = x_scales[0].bitcast(I32).rearrange("(q r) c -> r q c", r=4)
+        for r in range(4):
+            src = rows[r].unsqueeze(1).to_broadcast([4, 2, T // 4])
+            queue = nc.sync if r < 2 else nc.scalar
+            queue.dma_start(x_bytes[r:P:16, :].bitcast(I32), src)
         x_codes = sb.tile([P, T], U32, name="x_codes")
         nc.sync.dma_start(x_codes[:].bitcast(I32), x_words[0].rearrange("p c r -> p (c r)").bitcast(I32))
         w2_raw = [load_weight_half("wa%d" % h, w2, h) for h in range(2)]
-        gm_sb = sb.tile([P, PACK], F32, name="gm_sb")
-        nc.sync.dma_start(gm_sb[:], gm.rearrange("(p t) o -> p (t o)", t=PACK))
         n3_l = load_list("n3_l", n3)
         n4_l = load_list("n4_l", n4)
         w1_raw = [load_weight_half("wb%d" % h, w1, h) for h in range(2)]
@@ -107,41 +112,43 @@ def tile_picked_hjoinwindstdtrack_none_p_kernel(
         n1_l = load_list("n1_l", n1)
         n2_l = load_list("n2_l", n2)
 
-        ident = sb.tile([P, P], F32, name="ident")
-        make_identity(nc, ident[:])
-
-        hz_bytes = sb.tile([P, S], U8, name="hz_bytes", align_bytes=64)
-        nc.vector.tensor_copy(hz_bytes[:], x_bytes[:].indirect(hz_l[:]))
-        hz_scales = sb.tile([P, S], U8, name="hz_scales", align_bytes=64)
-        nc.vector.tensor_copy(hz_scales[:].bitcast(I32), hz_bytes[:].bitcast(I32))
-        for r in (2, 3):
-            nc.scalar.dma_start(hz_scales[r:P:32, :].bitcast(I32), hz_bytes[16 + r : P : 32, :].bitcast(I32))
-        offs_scales = sb.tile([P, S], U8, name="offs_scales", align_bytes=64)
-        nc.vector.tensor_copy(offs_scales[:], x_bytes[:].indirect(offs_l[:]))
-
-        hz_codes = sb.tile([P, S], U32, name="hz_codes", tag="bytes_then_codes", align_bytes=64)
-        nc.vector.tensor_copy(hz_codes[:], x_codes[:].indirect(hz_l[:]))
-        offs_codes = sb.tile([P, S], U32, name="offs_codes", align_bytes=64)
-        nc.vector.tensor_copy(offs_codes[:], x_codes[:].indirect(offs_l[:]))
-
         gw = sb.tile([P, PACK], F32, name="gw")
         nc.vector.tensor_scalar(gw[:], gm_sb[:], 0.6875, None, ALU.mult)
         gzero = sb.tile([P, PACK], F32, name="gzero")
         nc.vector.tensor_scalar(gzero[:], gm_sb[:], 0.0, None, ALU.is_equal)
+        gsq = sb.tile([P, PACK], F32, name="gsq")
+        nc.vector.tensor_tensor(gsq[:], gw[:], gw[:], ALU.mult)
+        gsafe = sb.tile([P, PACK], F32, name="gsafe", tag="w2_g", align_bytes=64)
+        nc.vector.tensor_tensor(gsafe[:], gsq[:], gzero[:], ALU.add)
+        ginv = sb.tile([P, PACK], F32, name="ginv")
+        nc.scalar.activation(ginv[:], gsafe[:], ACT.Abs_reciprocal_sqrt)
+
+        ident = sb.tile([P, P], F32, name="ident")
+        make_identity(nc, ident[:])
+
+        hz_bytes = sb.tile([P, S], U8, name="hz_bytes", tag="picked_bytes", align_bytes=64)
+        nc.vector.tensor_copy(hz_bytes[:], x_bytes[:].indirect(hz_l[:]))
+        hz_scales = sb.tile([P, S], U8, name="hz_scales", align_bytes=64)
+        nc.vector.tensor_copy(hz_scales[:].bitcast(I32), hz_bytes[:].bitcast(I32))
+        for r in (2, 3):
+            nc.scalar.dma_start(hz_scales[r:P:32, :].bitcast(I32), hz_scales[16 + r : P : 32, :].bitcast(I32))
+        offs_scales = sb.tile([P, S], U8, name="offs_scales", tag="picked_bytes", align_bytes=64)
+        nc.vector.tensor_copy(offs_scales[:], x_bytes[:].indirect(offs_l[:]))
+
+        hz_codes = sb.tile([P, S], U32, name="hz_codes", tag="bytes_then_codes", align_bytes=64)
+        nc.vector.tensor_copy(hz_codes[:], x_codes[:].indirect(hz_l[:]))
         w2_g = sb.tile([P, 2048], BF16, name="w2_g", align_bytes=64)
-        round_dealt(w2_g, w2_raw[0], 0, "scalar")
-        round_dealt(w2_g, w2_raw[1], 1, "vector")
+        round_dealt(w2_g, w2_raw, 0, "scalar")
+        round_dealt(w2_g, w2_raw, 1, "vector")
         w2_q = quantize("w2", w2_g, 2)
+        offs_codes = sb.tile([P, S], U32, name="offs_codes", tag="wa1", align_bytes=64)
+        nc.vector.tensor_copy(offs_codes[:], x_codes[:].indirect(offs_l[:]))
         d_acc = []
         for t in range(PACK):
             acc = ps.tile([P, S], F32, name="d_acc", tag="bank")
             mx(acc[:], w2_q, blk(t), (hz_codes, hz_scales), slice(0, S))
             d_acc.append(acc)
 
-        gsafe = sb.tile([P, PACK], F32, name="gsafe")
-        nc.vector.tensor_tensor(gsafe[:], gw[:], gzero[:], ALU.add)
-        ginv = sb.tile([P, PACK], F32, name="ginv")
-        nc.vector.reciprocal(ginv[:], gsafe[:])
         qscale = sb.tile([P, PACK], F32, name="qscale")
         nc.vector.scalar_tensor_tensor(qscale[:], ginv[:], 0.1953125, ginv[:], ALU.mult, ALU.mult)
         quarter = sb.tile([P, 1], F32, name="quarter")
@@ -172,7 +179,10 @@ def tile_picked_hjoinwindstdtrack_none_p_kernel(
             a = ring.tile([P, HALF], F32, name="a")
             b = ring.tile([P, HALF], F32, name="b")
             nc.scalar.activation(a[:], win[:].indirect(half_list(n3_l, h)), ACT.Copy, scale=-0.6)
-            nc.vector.tensor_scalar(b[:], win[:].indirect(half_list(n4_l, h)), 0.6, 0.0, ALU.mult, ALU.add)
+            if (t, h) in B_ON_SCALAR:
+                nc.scalar.activation(b[:], win[:].indirect(half_list(n4_l, h)), ACT.Copy, scale=0.6)
+            else:
+                nc.vector.tensor_scalar(b[:], win[:].indirect(half_list(n4_l, h)), 0.6, 0.0, ALU.mult, ALU.add)
             s = ring.tile([P, HALF], F32, name="s")
             nc.vector.tensor_tensor(s[:], a[:], b[:], ALU.subtract)
             tu_acc = ps.tile([P, 2, HALF], F32, name="tu_acc", tag="bank")
@@ -196,12 +206,17 @@ def tile_picked_hjoinwindstdtrack_none_p_kernel(
                 rinv[:, t, half_cols(h)], q_acc[:], ACT.Abs_reciprocal_sqrt, bias=quarter[:], scale=qscale[:, t : t + 1]
             )
 
-        def wind(t, h):
-            y1 = ring.tile([P, HALF], F32, name="y1", bufs=2)
-            y2 = ring.tile([P, HALF], F32, name="y2", bufs=2)
-            nc.scalar.activation(y1[:], y_win[:, t, :].indirect(half_list(n1_l, h)), ACT.Copy)
-            nc.scalar.activation(y2[:], y_win[:, t, :].indirect(half_list(n2_l, h)), ACT.Copy)
-            nc.vector.tensor_tensor(diff[:, t, half_cols(h)], y1[:], y2[:], ALU.subtract)
+        def wind(t, c0, c1, second):
+            width = (c1 - c0) * P
+            part = slice(c0 * P // 16, c1 * P // 16)
+            y1 = ring.tile([P, width], F32, name="y1", bufs=3)
+            y2 = ring.tile([P, width], F32, name="y2", bufs=3)
+            nc.scalar.activation(y1[:], y_win[:, t, :].indirect(n1_l[:, part]), ACT.Copy)
+            if second == "vector":
+                nc.vector.tensor_copy(y2[:], y_win[:, t, :].indirect(n2_l[:, part]))
+            else:
+                nc.scalar.activation(y2[:], y_win[:, t, :].indirect(n2_l[:, part]), ACT.Copy)
+            nc.vector.tensor_tensor(diff[:, t, c0 * P : c1 * P], y1[:], y2[:], ALU.subtract)
 
         def woven(ap):
             return ap.rearrange("p t (c i) -> p c t i", i=4)
@@ -209,11 +224,11 @@ def tile_picked_hjoinwindstdtrack_none_p_kernel(
         def weave(tile, c0, c1):
             return tile[:].rearrange("p (c i t) -> p c t i", i=4, t=PACK)[:, 32 * c0 : 32 * c1]
 
-        def quantize_half(q, grouped, h):
+        def quantize_cols(q, grouped, c0, c1):
             nc.vector.quantize_mx(
-                out=q[0][:, h * HALF : (h + 1) * HALF].bitcast(FP8X4),
-                scales=q[1][:, h * HALF : (h + 1) * HALF],
-                in_=grouped[:, h * 1024 : (h + 1) * 1024],
+                out=q[0][:, c0 * P : c1 * P].bitcast(FP8X4),
+                scales=q[1][:, c0 * P : c1 * P],
+                in_=grouped[:, PACK * c0 * P : PACK * c1 * P],
             )
 
         w4_g = sb.tile([P, 2048], BF16, name="w4_g", align_bytes=64)
@@ -233,8 +248,8 @@ def tile_picked_hjoinwindstdtrack_none_p_kernel(
 
         def project_y():
             w1_g = sb.tile([P, 2048], BF16, name="w1_g", align_bytes=64)
-            round_dealt(w1_g, w1_raw[0], 0, "scalar")
-            round_dealt(w1_g, w1_raw[1], 1, "vector")
+            round_dealt(w1_g, w1_raw, 0, "scalar")
+            round_dealt(w1_g, w1_raw, 1, "vector")
             w1_q = quantize("w1", w1_g)
             for c in range(4):
                 acc = ps_y.tile([P, PACK, P], F32, name="y_acc")
@@ -245,75 +260,106 @@ def tile_picked_hjoinwindstdtrack_none_p_kernel(
                 )
                 y_acc.append(acc)
 
-        def wind_product(h):
-            for c in (2 * h, 2 * h + 1):
-                nc.vector.tensor_tensor(weave(z_g, c, c + 1), woven(y_acc[c][:]), woven(diff[:, :, blk(c)]), ALU.mult)
+        def wind_product(c):
+            nc.vector.tensor_tensor(weave(z_g, c, c + 1), woven(y_acc[c][:]), woven(diff[:, :, blk(c)]), ALU.mult)
 
         def track_product(h):
             cols = half_cols(h)
             nc.vector.tensor_tensor(weave(z2_g, 2 * h, 2 * h + 2), woven(num[:, :, cols]), woven(rinv[:, :, cols]), ALU.mult)
 
+        h_win = [sb.tile([P, S], F32, name="h_win%d" % m) for m in range(4)]
+
+        def join(acc, m, cols, first, last):
+            if first:
+                mx(acc, w4_q, blk(m), z2_q, cols, True, False)
+            if last:
+                mx(acc, w3_q, blk(m), z_q, cols, False, True)
+
         units = [(t, h) for h in range(2) for t in range(PACK)]
+        winds = [(t, 0, 2, W0[t]) for t in range(PACK)] + [(t, c, c + 1, W1[t]) for c in (2, 3) for t in range(PACK)]
         fronts, sums = {}, {}
         for step in range(len(units) + 4):
             if step < len(units):
                 fronts[step] = track_front(*units[step])
             if step == 1:
                 project_y()
-                w4_raw = [load_weight_half("wa%d" % h, w4, h) for h in range(2)]
+                w4_raw = [load_weight_half(name, w4, h) for h, name in enumerate(("wa0", "w2_g"))]
                 w3_raw = [load_weight_half("wb%d" % h, w3, h) for h in range(2)]
                 n5_l = load_list("n5_l", n5)
                 n6_l = load_list("n6_l", n6)
             if 0 <= step - 2 < len(units):
                 sums[step - 2] = track_back(*units[step - 2], *fronts[step - 2])
-            if 0 <= step - 4 < len(units):
-                wind(*units[step - 4])
+            if 0 <= step - 4 < 4:
+                wind(*winds[step - 4])
+            if step in (8, 9):
+                wind(*winds[2 * step - 12])
+                wind(*winds[2 * step - 11])
             if 0 <= step - 3 < len(units):
                 track_root(*units[step - 3], sums[step - 3])
-            if step == 5:
+            if step == 4:
                 for h in range(2):
-                    round_plain(w4_g, w4_raw[h], h, "vector")
-            if step == 6:
+                    round_plain(w4_g, w4_raw, h, "vector")
+            if step == 5:
                 w4_q = quantize("w4", w4_g)
+                for h in range(2):
+                    round_plain(w3_g, w3_raw, h, "vector")
+            if step == 6:
+                w3_q = quantize("w3", w3_g)
             if step == 7:
                 track_product(0)
             if step == 8:
                 wind_product(0)
-                quantize_half(z2_q, z2_g, 0)
+                quantize_cols(z2_q, z2_g, 0, 2)
+                wind_product(1)
             if step == 9:
-                for h in range(2):
-                    round_plain(w3_g, w3_raw[h], h, "vector")
-                quantize_half(z_q, z_g, 0)
+                quantize_cols(z_q, z_g, 0, 2)
             if step == 10:
-                w3_q = quantize("w3", w3_g)
                 track_product(1)
-        quantize_half(z2_q, z2_g, 1)
-        wind_product(1)
-        quantize_half(z_q, z_g, 1)
-
-        h_acc = []
+                wind_product(2)
+                quantize_cols(z2_q, z2_g, 2, 4)
+                for w in winds[8:10]:
+                    wind(*w)
+                quantize_cols(z_q, z_g, 2, 3)
+                for w in winds[10:12]:
+                    wind(*w)
+        wind_product(3)
+        early = []
+        for pair in range(2):
+            acc = ps_y.tile([P, 2, HALF], F32, name="h_early", tag="y_acc")
+            for i in range(2):
+                join(acc[:, i, :], 2 * pair + i, half_cols(0), True, True)
+            early.append(acc)
+        late = []
         for m in range(4):
-            acc = ps.tile([P, S], F32, name="h_acc", tag="bank")
-            mx(acc[:], w4_q, blk(m), z2_q, slice(0, S), True, False)
-            h_acc.append(acc)
+            acc = ps.tile([P, 2, P], F32, name="h_late", tag="bank")
+            join(acc[:, 0, :], m, blk(2), True, True)
+            join(acc[:, 1, :], m, blk(3), True, False)
+            late.append(acc)
+        quantize_cols(z_q, z_g, 3, 4)
         for m in range(4):
-            mx(h_acc[m][:], w3_q, blk(m), z_q, slice(0, S), False, True)
+            nc.scalar.copy(h_win[m][:, half_cols(0)], early[m // 2][:, m % 2, :])
         for m in range(4):
-            h_win = sb.tile([P, S], F32, name="h_win%d" % m)
-            nc.vector.tensor_copy(h_win[:], h_acc[m][:])
+            join(late[m][:, 1, :], m, blk(3), False, True)
+        for m in range(4):
+            nc.vector.tensor_copy(h_win[m][:, half_cols(1)], late[m][:].rearrange("p c j -> p (c j)"))
+        for m in range(4):
+            win = h_win[m]
             gate = ring.tile([P, S], F32, name="gate")
             far = ring.tile([P, S], F32, name="far")
             step = ring.tile([P, S], F32, name="step")
             gated = ring.tile([P, S], F32, name="gated")
             res = sb.tile([P, S], F32, name="res%d" % m)
-            halves = [slice(h * HALF, (h + 1) * HALF) for h in range(2)]
+            halves = [half_cols(h) for h in range(2)]
             for h, cols in enumerate(halves):
-                nc.scalar.activation(gate[:, cols], h_win[:].indirect(half_list(n5_l, h)), ACT.Sigmoid)
-                nc.scalar.activation(far[:, cols], h_win[:].indirect(half_list(n6_l, h)), ACT.Copy)
+                if (m, h) in FAR_ON_VECTOR:
+                    nc.vector.tensor_copy(far[:, cols], win[:].indirect(half_list(n6_l, h)))
+                else:
+                    nc.scalar.activation(far[:, cols], win[:].indirect(half_list(n6_l, h)), ACT.Copy)
+                nc.scalar.activation(gate[:, cols], win[:].indirect(half_list(n5_l, h)), ACT.Sigmoid)
             for cols in halves:
-                nc.vector.tensor_tensor(step[:, cols], far[:, cols], h_win[:, cols], ALU.subtract)
+                nc.vector.tensor_tensor(step[:, cols], far[:, cols], win[:, cols], ALU.subtract)
             for cols in halves:
                 nc.vector.tensor_tensor(gated[:, cols], step[:, cols], gate[:, cols], ALU.mult)
             for cols in halves:
-                nc.vector.tensor_tensor(res[:, cols], gated[:, cols], h_win[:, cols], ALU.add)
+                nc.vector.tensor_tensor(res[:, cols], gated[:, cols], win[:, cols], ALU.add)
                 nc.sync.dma_start(out[blk(m), cols], res[:, cols])

from contextlib import ExitStack

import concourse.mybir as mybir
from concourse.masks import make_identity

K, T, S, N, H = 512, 2048, 512, 512, 512
FLOPS = 4 * 2 * 512 * 512 * 512

F32 = mybir.dt.float32
BF16 = mybir.dt.bfloat16
I32 = mybir.dt.int32
U32 = mybir.dt.uint32
U16 = mybir.dt.uint16
U8 = mybir.dt.uint8
FP8X4 = mybir.dt.float8_e4m3fn_x4
ACT = mybir.ActivationFunctionType
ALU = mybir.AluOpType

P = 128
PACK = 4
HALF = S // 2
W0 = ["vector", "scalar", "scalar", "scalar"]
W1 = ["scalar", "scalar", "scalar", "scalar"]
B_ON_SCALAR = [(3, 1)]
FAR_ON_VECTOR = [(0, 0), (2, 0)]


def tile_picked_hjoinwindstdtrack_none_p_kernel(
    tc, x_words, x_scales, w1, w2, gn, gm, w3, w4, offs, hz, n1, n2, n3, n4, n5, n6, out
):
    nc = tc.nc
    with ExitStack() as ctx:
        sb = ctx.enter_context(tc.tile_pool(name="sb", bufs=1))
        ring = ctx.enter_context(tc.tile_pool(name="ring", bufs=4))
        ps = ctx.enter_context(tc.psum_pool(name="ps", bufs=4))
        ps_y = ctx.enter_context(tc.psum_pool(name="ps_y", bufs=4))

        def load_list(name, src):
            tile = sb.tile([P, S // 16], U16, name=name)
            nc.sync.dma_start(tile[:], src)
            return tile

        def load_weight_half(name, w, half):
            raw = sb.tile([P, PACK, HALF], F32, name=name, align_bytes=64)
            cols = slice(half * HALF, (half + 1) * HALF)
            nc.sync.dma_start(raw[:], w.rearrange("(p j) c -> p j c", j=PACK)[:, :, cols])
            return raw

        def half_list(tile, half):
            return tile[:, half * HALF // 16 : (half + 1) * HALF // 16]

        def copy_on(engine, dst, src):
            if engine == "scalar":
                nc.scalar.copy(dst, src)
            else:
                nc.vector.tensor_copy(dst, src)

        def round_dealt(grouped, raw, half, engine):
            dst = grouped[:].rearrange("p (t m j) -> p m j t", t=PACK, j=PACK)[:, half * 64 : (half + 1) * 64]
            copy_on(engine, dst, raw[half][:].rearrange("p j (m t) -> p m j t", t=PACK))

        def round_plain(grouped, raw, half, engine):
            dst = grouped[:].rearrange("p (c i j) -> p c j i", i=4, j=PACK)[:, half * 64 : (half + 1) * 64]
            copy_on(engine, dst, raw[half][:].rearrange("p j (c i) -> p c j i", i=4))

        def quantize(name, grouped, pieces=1):
            codes = sb.tile([P, 512], U32, name=name + "_codes", align_bytes=64)
            scales = sb.tile([P, 512], U8, name=name + "_scales", align_bytes=64)
            width = 512 // pieces
            for i in range(pieces):
                cols = slice(i * width, (i + 1) * width)
                nc.vector.quantize_mx(
                    out=codes[:, cols].bitcast(FP8X4),
                    scales=scales[:, cols],
                    in_=grouped[:, PACK * i * width : PACK * (i + 1) * width],
                )
            return codes, scales

        def mx(acc, lhs, lcols, rhs, rcols, start=True, stop=True):
            nc.tensor.matmul_mx(
                out=acc,
                lhsT=lhs[0][:, lcols].bitcast(FP8X4),
                lhsT_scale=lhs[1][:, lcols],
                rhs=rhs[0][:, rcols].bitcast(FP8X4),
                rhs_scale=rhs[1][:, rcols],
                start=start,
                stop=stop,
            )

        def blk(i):
            return slice(i * P, (i + 1) * P)

        x_bytes = sb.tile([P, T], U8, name="x_bytes", tag="bytes_then_codes", align_bytes=64)
        nc.gpsimd.memset(x_bytes[:].bitcast(I32), 0)
        hz_l = load_list("hz_l", hz)
        gm_sb = sb.tile([P, PACK], F32, name="gm_sb")
        nc.scalar.dma_start(gm_sb[:], gm.rearrange("(p t) o -> p (t o)", t=PACK))
        offs_l = load_list("offs_l", offs)
        rows = x_scales[0].bitcast(I32).rearrange("(q r) c -> r q c", r=4)
        for r in range(4):
            src = rows[r].unsqueeze(1).to_broadcast([4, 2, T // 4])
            queue = nc.sync if r < 2 else nc.scalar
            queue.dma_start(x_bytes[r:P:16, :].bitcast(I32), src)
        x_codes = sb.tile([P, T], U32, name="x_codes")
        nc.sync.dma_start(x_codes[:].bitcast(I32), x_words[0].rearrange("p c r -> p (c r)").bitcast(I32))
        w2_raw = [load_weight_half("wa%d" % h, w2, h) for h in range(2)]
        n3_l = load_list("n3_l", n3)
        n4_l = load_list("n4_l", n4)
        w1_raw = [load_weight_half("wb%d" % h, w1, h) for h in range(2)]
        gn_sb = sb.tile([P, PACK], F32, name="gn_sb")
        nc.sync.dma_start(gn_sb[:], gn.rearrange("(p t) o -> p (t o)", t=PACK))
        n1_l = load_list("n1_l", n1)
        n2_l = load_list("n2_l", n2)

        gw = sb.tile([P, PACK], F32, name="gw")
        nc.vector.tensor_scalar(gw[:], gm_sb[:], 0.6875, None, ALU.mult)
        gzero = sb.tile([P, PACK], F32, name="gzero")
        nc.vector.tensor_scalar(gzero[:], gm_sb[:], 0.0, None, ALU.is_equal)
        gsq = sb.tile([P, PACK], F32, name="gsq")
        nc.vector.tensor_tensor(gsq[:], gw[:], gw[:], ALU.mult)
        gsafe = sb.tile([P, PACK], F32, name="gsafe", tag="w2_g", align_bytes=64)
        nc.vector.tensor_tensor(gsafe[:], gsq[:], gzero[:], ALU.add)
        ginv = sb.tile([P, PACK], F32, name="ginv")
        nc.scalar.activation(ginv[:], gsafe[:], ACT.Abs_reciprocal_sqrt)

        ident = sb.tile([P, P], F32, name="ident")
        make_identity(nc, ident[:])

        hz_bytes = sb.tile([P, S], U8, name="hz_bytes", tag="picked_bytes", align_bytes=64)
        nc.vector.tensor_copy(hz_bytes[:], x_bytes[:].indirect(hz_l[:]))
        hz_scales = sb.tile([P, S], U8, name="hz_scales", align_bytes=64)
        nc.vector.tensor_copy(hz_scales[:].bitcast(I32), hz_bytes[:].bitcast(I32))
        for r in (2, 3):
            nc.scalar.dma_start(hz_scales[r:P:32, :].bitcast(I32), hz_scales[16 + r : P : 32, :].bitcast(I32))
        offs_scales = sb.tile([P, S], U8, name="offs_scales", tag="picked_bytes", align_bytes=64)
        nc.vector.tensor_copy(offs_scales[:], x_bytes[:].indirect(offs_l[:]))

        hz_codes = sb.tile([P, S], U32, name="hz_codes", tag="bytes_then_codes", align_bytes=64)
        nc.vector.tensor_copy(hz_codes[:], x_codes[:].indirect(hz_l[:]))
        w2_g = sb.tile([P, 2048], BF16, name="w2_g", align_bytes=64)
        round_dealt(w2_g, w2_raw, 0, "scalar")
        round_dealt(w2_g, w2_raw, 1, "vector")
        w2_q = quantize("w2", w2_g, 2)
        offs_codes = sb.tile([P, S], U32, name="offs_codes", tag="wa1", align_bytes=64)
        nc.vector.tensor_copy(offs_codes[:], x_codes[:].indirect(offs_l[:]))
        d_acc = []
        for t in range(PACK):
            acc = ps.tile([P, S], F32, name="d_acc", tag="bank")
            mx(acc[:], w2_q, blk(t), (hz_codes, hz_scales), slice(0, S))
            d_acc.append(acc)

        qscale = sb.tile([P, PACK], F32, name="qscale")
        nc.vector.scalar_tensor_tensor(qscale[:], ginv[:], 0.1953125, ginv[:], ALU.mult, ALU.mult)
        quarter = sb.tile([P, 1], F32, name="quarter")
        nc.vector.memset(quarter[:], 0.25)

        num = sb.tile([P, PACK, S], F32, name="num")
        rinv = sb.tile([P, PACK, S], F32, name="rinv")
        diff = sb.tile([P, PACK, S], F32, name="diff")

        d_win = [sb.tile([P, S], F32, name="d_win%d" % t) for t in range(PACK)]
        y_win = sb.tile([P, PACK, S], F32, name="y_win")

        def turned_sum(acc, terms):
            for c in range(2):
                for i, term in enumerate(terms):
                    nc.tensor.matmul(
                        acc[:, blk(c)], term[:, blk(c)], ident[:],
                        start=(i == 0), stop=(i == len(terms) - 1), is_transpose=True,
                    )

        def half_cols(h):
            return slice(h * HALF, (h + 1) * HALF)

        def track_front(t, h):
            win = d_win[t]
            if h == 0:
                nc.scalar.activation(win[:], d_acc[t][:], ACT.Copy, scale=gw[:, t : t + 1])
            a = ring.tile([P, HALF], F32, name="a")
            b = ring.tile([P, HALF], F32, name="b")
            nc.scalar.activation(a[:], win[:].indirect(half_list(n3_l, h)), ACT.Copy, scale=-0.6)
            if (t, h) in B_ON_SCALAR:
                nc.scalar.activation(b[:], win[:].indirect(half_list(n4_l, h)), ACT.Copy, scale=0.6)
            else:
                nc.vector.tensor_scalar(b[:], win[:].indirect(half_list(n4_l, h)), 0.6, 0.0, ALU.mult, ALU.add)
            s = ring.tile([P, HALF], F32, name="s")
            nc.vector.tensor_tensor(s[:], a[:], b[:], ALU.subtract)
            tu_acc = ps.tile([P, 2, HALF], F32, name="tu_acc", tag="bank")
            turned_sum(tu_acc[:, 0, :], [a, b])
            turned_sum(tu_acc[:, 1, :], [s, win[:, half_cols(h)]])
            return tu_acc, s

        def track_back(t, h, tu_acc, s):
            cols = half_cols(h)
            nc.vector.scalar_tensor_tensor(num[:, t, cols], s[:], 25.0 / 33.0, d_win[t][:, cols], ALU.mult, ALU.add)
            t2 = ring.tile([P, HALF], F32, name="t2")
            nc.scalar.activation(t2[:], tu_acc[:, 0, :], ACT.Square, scale=8.0 / 3.0)
            u2 = ring.tile([P, HALF], F32, name="u2")
            nc.scalar.activation(u2[:], tu_acc[:, 1, :], ACT.Square)
            q_acc = ps.tile([P, HALF], F32, name="q_acc", tag="bank")
            turned_sum(q_acc, [t2, u2])
            return q_acc

        def track_root(t, h, q_acc):
            nc.scalar.activation(
                rinv[:, t, half_cols(h)], q_acc[:], ACT.Abs_reciprocal_sqrt, bias=quarter[:], scale=qscale[:, t : t + 1]
            )

        def wind(t, c0, c1, second):
            width = (c1 - c0) * P
            part = slice(c0 * P // 16, c1 * P // 16)
            y1 = ring.tile([P, width], F32, name="y1", bufs=3)
            y2 = ring.tile([P, width], F32, name="y2", bufs=3)
            nc.scalar.activation(y1[:], y_win[:, t, :].indirect(n1_l[:, part]), ACT.Copy)
            if second == "vector":
                nc.vector.tensor_copy(y2[:], y_win[:, t, :].indirect(n2_l[:, part]))
            else:
                nc.scalar.activation(y2[:], y_win[:, t, :].indirect(n2_l[:, part]), ACT.Copy)
            nc.vector.tensor_tensor(diff[:, t, c0 * P : c1 * P], y1[:], y2[:], ALU.subtract)

        def woven(ap):
            return ap.rearrange("p t (c i) -> p c t i", i=4)

        def weave(tile, c0, c1):
            return tile[:].rearrange("p (c i t) -> p c t i", i=4, t=PACK)[:, 32 * c0 : 32 * c1]

        def quantize_cols(q, grouped, c0, c1):
            nc.vector.quantize_mx(
                out=q[0][:, c0 * P : c1 * P].bitcast(FP8X4),
                scales=q[1][:, c0 * P : c1 * P],
                in_=grouped[:, PACK * c0 * P : PACK * c1 * P],
            )

        w4_g = sb.tile([P, 2048], BF16, name="w4_g", align_bytes=64)
        w3_g = sb.tile([P, 2048], BF16, name="w3_g", align_bytes=64)
        z2_g = sb.tile([P, 2048], BF16, name="z2_g", align_bytes=64)
        z_g = sb.tile([P, 2048], BF16, name="z_g", align_bytes=64)
        z_q = (
            sb.tile([P, 512], U32, name="z_codes", align_bytes=64),
            sb.tile([P, 512], U8, name="z_scales", align_bytes=64),
        )

        z2_q = (
            sb.tile([P, 512], U32, name="z2_codes", align_bytes=64),
            sb.tile([P, 512], U8, name="z2_scales", align_bytes=64),
        )
        y_acc = []

        def project_y():
            w1_g = sb.tile([P, 2048], BF16, name="w1_g", align_bytes=64)
            round_dealt(w1_g, w1_raw, 0, "scalar")
            round_dealt(w1_g, w1_raw, 1, "vector")
            w1_q = quantize("w1", w1_g)
            for c in range(4):
                acc = ps_y.tile([P, PACK, P], F32, name="y_acc")
                for t in range(PACK):
                    mx(acc[:, t, :], w1_q, blk(t), (offs_codes, offs_scales), blk(c))
                nc.vector.tensor_tensor(
                    y_win[:, :, blk(c)], acc[:], gn_sb[:].unsqueeze(2).to_broadcast([P, PACK, P]), ALU.mult
                )
                y_acc.append(acc)

        def wind_product(c):
            nc.vector.tensor_tensor(weave(z_g, c, c + 1), woven(y_acc[c][:]), woven(diff[:, :, blk(c)]), ALU.mult)

        def track_product(h):
            cols = half_cols(h)
            nc.vector.tensor_tensor(weave(z2_g, 2 * h, 2 * h + 2), woven(num[:, :, cols]), woven(rinv[:, :, cols]), ALU.mult)

        h_win = [sb.tile([P, S], F32, name="h_win%d" % m) for m in range(4)]

        def join(acc, m, cols, first, last):
            if first:
                mx(acc, w4_q, blk(m), z2_q, cols, True, False)
            if last:
                mx(acc, w3_q, blk(m), z_q, cols, False, True)

        units = [(t, h) for h in range(2) for t in range(PACK)]
        winds = [(t, 0, 2, W0[t]) for t in range(PACK)] + [(t, c, c + 1, W1[t]) for c in (2, 3) for t in range(PACK)]
        fronts, sums = {}, {}
        for step in range(len(units) + 4):
            if step < len(units):
                fronts[step] = track_front(*units[step])
            if step == 1:
                project_y()
                w4_raw = [load_weight_half(name, w4, h) for h, name in enumerate(("wa0", "w2_g"))]
                w3_raw = [load_weight_half("wb%d" % h, w3, h) for h in range(2)]
                n5_l = load_list("n5_l", n5)
                n6_l = load_list("n6_l", n6)
            if 0 <= step - 2 < len(units):
                sums[step - 2] = track_back(*units[step - 2], *fronts[step - 2])
            if 0 <= step - 4 < 4:
                wind(*winds[step - 4])
            if step in (8, 9):
                wind(*winds[2 * step - 12])
                wind(*winds[2 * step - 11])
            if 0 <= step - 3 < len(units):
                track_root(*units[step - 3], sums[step - 3])
            if step == 4:
                for h in range(2):
                    round_plain(w4_g, w4_raw, h, "vector")
            if step == 5:
                w4_q = quantize("w4", w4_g)
                for h in range(2):
                    round_plain(w3_g, w3_raw, h, "vector")
            if step == 6:
                w3_q = quantize("w3", w3_g)
            if step == 7:
                track_product(0)
            if step == 8:
                wind_product(0)
                quantize_cols(z2_q, z2_g, 0, 2)
                wind_product(1)
            if step == 9:
                quantize_cols(z_q, z_g, 0, 2)
            if step == 10:
                track_product(1)
                wind_product(2)
                quantize_cols(z2_q, z2_g, 2, 4)
                for w in winds[8:10]:
                    wind(*w)
                quantize_cols(z_q, z_g, 2, 3)
                for w in winds[10:12]:
                    wind(*w)
        wind_product(3)
        early = []
        for pair in range(2):
            acc = ps_y.tile([P, 2, HALF], F32, name="h_early", tag="y_acc")
            for i in range(2):
                join(acc[:, i, :], 2 * pair + i, half_cols(0), True, True)
            early.append(acc)
        late = []
        for m in range(4):
            acc = ps.tile([P, 2, P], F32, name="h_late", tag="bank")
            join(acc[:, 0, :], m, blk(2), True, True)
            join(acc[:, 1, :], m, blk(3), True, False)
            late.append(acc)
        quantize_cols(z_q, z_g, 3, 4)
        for m in range(4):
            nc.scalar.copy(h_win[m][:, half_cols(0)], early[m // 2][:, m % 2, :])
        for m in range(4):
            join(late[m][:, 1, :], m, blk(3), False, True)
        for m in range(4):
            nc.vector.tensor_copy(h_win[m][:, half_cols(1)], late[m][:].rearrange("p c j -> p (c j)"))
        for m in range(4):
            win = h_win[m]
            gate = ring.tile([P, S], F32, name="gate")
            far = ring.tile([P, S], F32, name="far")
            step = ring.tile([P, S], F32, name="step")
            gated = ring.tile([P, S], F32, name="gated")
            res = sb.tile([P, S], F32, name="res%d" % m)
            halves = [half_cols(h) for h in range(2)]
            for h, cols in enumerate(halves):
                if (m, h) in FAR_ON_VECTOR:
                    nc.vector.tensor_copy(far[:, cols], win[:].indirect(half_list(n6_l, h)))
                else:
                    nc.scalar.activation(far[:, cols], win[:].indirect(half_list(n6_l, h)), ACT.Copy)
                nc.scalar.activation(gate[:, cols], win[:].indirect(half_list(n5_l, h)), ACT.Sigmoid)
            for cols in halves:
                nc.vector.tensor_tensor(step[:, cols], far[:, cols], win[:, cols], ALU.subtract)
            for cols in halves:
                nc.vector.tensor_tensor(gated[:, cols], step[:, cols], gate[:, cols], ALU.mult)
            for cols in halves:
                nc.vector.tensor_tensor(res[:, cols], gated[:, cols], win[:, cols], ALU.add)
                nc.sync.dma_start(out[blk(m), cols], res[:, cols])
